import numpy as np, ml_dtypes
CORES = [30,158,46,174,86,214]
N = 6
T, SQ = 4096, 2048
def entries(a): return a.T.reshape(-1)
def pack(v, P): return np.ascontiguousarray(np.asarray(v, np.int32).reshape(-1, P).T)
def lists(rng, how):
    d = np.concatenate([[0], rng.integers(1 - SQ // 2, SQ // 2, N - 1), [int(rng.integers(1 - SQ // 2, 1))]])
    if how == "lag": d[1:] = -SQ
    if how == "lead": d[1:N] = SQ; d[N] = 0
    if how == "runs": m = int(rng.integers(1, N - 2)); d[m] = -abs(d[m]); d[m + 1] = d[m] + SQ; d[m + 2] = d[m]
    if how == "skew": t = int(rng.integers(2, N - 1)); d[1:] = rng.integers(SQ // 2 + 1, SQ - 1, N); d[t + 1:] *= -1; d[t] = d[t - 1] + d[t + 1]
    n = SQ + np.diff(d)
    F = np.zeros((N, T), np.int64)
    for r in range(N):
        o = rng.permutation(T)
        if how == "runs": o = (T // 16 * rng.permutation(16)[:, None] + np.arange(T // 16)).reshape(-1)
        if how == "skew": o = np.concatenate([[0, T - 1], 1 + rng.permutation(T - 2)])
        F[r, o[:n[r]]] = 1
    return {"fl": np.stack([pack(f, 16) for f in F])}
def setup_inputs(rng):
    return dict({"x": rng.standard_normal((N, 128, T), dtype=np.float32).astype(ml_dtypes.bfloat16), "st": rng.standard_normal((N, 128, SQ), dtype=np.float32).astype(ml_dtypes.bfloat16)}, **lists(rng, "uniform"))
def setup_inputs_lag(rng):
    d = setup_inputs(rng); d.update(lists(rng, "lag"))
    for k in ("x", "st"): d[k] = (d[k].astype(np.float32) * 1048576.0).astype(d[k].dtype)
    return d
def setup_inputs_lead(rng):
    d = setup_inputs(rng); d.update(lists(rng, "lead"))
    for k in ("x", "st"): d[k] = (d[k].astype(np.float32) * (1 / 1024.0)).astype(d[k].dtype)
    return d
def setup_inputs_runs(rng):
    d = setup_inputs(rng); d.update(lists(rng, "runs"))
    return d
def setup_inputs_skew(rng):
    d = setup_inputs(rng); d.update(lists(rng, "skew"))
    return d
def check_inputs(x):
    bad = []
    if x["fl"].min() < 0 or x["fl"].max() >= 2: bad.append("fl out of range")
    if int(x["fl"].sum()) > N * SQ: bad.append("more flags than the stream has columns")
    c = np.concatenate([[0], np.cumsum([int(a.sum()) for a in x["fl"]])])
    if any(c[r] < (r - 1) * SQ or c[r + 1] > (r + 2) * SQ for r in range(N)): bad.append("a rank's share of the stream reaches beyond its neighbours' parts")
    return bad
def reference(x, st, fl):
    S = np.concatenate(list(st), axis=1); X = np.concatenate(list(x), axis=1)
    F = np.concatenate([entries(f) for f in fl]) > 0; c = np.cumsum(F) - F
    Y = np.where(F[None, :], S[:, np.minimum(c, N * SQ - 1)], X)
    return {"y": np.stack([Y[:, T * r:T * r + T] for r in range(N)])}

@@ -1,0 +1,169 @@
+from concourse.bass import DstId, RemoteDMATransfer
+from concourse.mybir import AluOpType, AxisListType, ActivationFunctionType
+
+NR = 6
+TC, SQ = 4096, 2048
+LC = TC // 16
+ROUNDS = [1536, 1536, 1024]
+
+SCRATCH = {
+    "win": ("sbuf", [128, TC + 3 * SQ], "bfloat16"),
+    "ot": ("sbuf", [128, TC], "bfloat16"),
+    "fsb": ("sbuf", [16, LC], "int32"),
+    "fb": ("sbuf", [16, LC + 16], "bfloat16"),
+    "pq": ("sbuf", [16, 128], "float32"),
+    "mge": ("sbuf", [16, 128], "bfloat16"),
+    "mlt": ("sbuf", [16, 128], "bfloat16"),
+    "meq": ("sbuf", [16, 128], "bfloat16"),
+    "pidx": ("sbuf", [128, 1], "int32"),
+    "pmod": ("sbuf", [128, 1], "int32"),
+    "pmodf": ("sbuf", [128, 1], "float32"),
+    "kx": ("sbuf", [128, LC], "float32"),
+    "zero": ("sbuf", [128, LC], "float32"),
+    "ones": ("sbuf", [128, 128], "float32"),
+    "tb": ("sbuf", [128, LC], "float32"),
+    "hh": ("sbuf", [128, LC], "float32"),
+    "off": ("sbuf", [128, LC], "uint16"),
+    "fe": ("sbuf", [128, 32 * (NR - 1)], "int32"),
+    "fef": ("sbuf", [128, 32 * (NR - 1)], "bfloat16"),
+    "fes": ("sbuf", [128, 1], "float32"),
+    "fd": ("dram", [128, 32], "int32"),
+    "flin": ("dram", [128 * (NR - 1), 32], "int32"),
+    "pd": ("psum", [128, 512], "float32"),
+    "pf": ("psum", [128, 512], "float32"),
+    "pe": ("psum", [128, 512], "float32"),
+    "pc": ("psum", [128, 512], "float32"),
+}
+SEMAPHORES = ["flc", "fls", "stl", "xl", "xgo", "arr", "arf", "fel", "snd", "gi", "v", "t", "tc", "o0", "o1", "o2", "ys"]
+
+
+def engines(mask):
+    return [i for i in range(16) if (mask >> i) & 1]
+
+
+def st_place(rank, src):
+    return TC + SQ * (src - max(rank - 1, 0))
+
+
+def rank_program(g, core, T, topo):
+    rank = T.rank_of(core)
+    if rank is None:
+        return
+    S = T.sem
+    W = TC + SQ * (3 - (rank == 0) - (rank == NR - 1))
+    own = st_place(rank, rank)
+    near = [r for r in (rank + 1, rank - 1) if 0 <= r < NR]
+    later = list(range(rank + 1, NR))
+
+    def did(r):
+        rid, pid = topo.addr(T.cores[r], core)
+        return DstId(rid=rid, pnc=pid)
+
+    def mask(rs):
+        m = topo.mask(core, T.cores[rs[0]])
+        for r in rs:
+            m &= topo.mask(core, T.cores[r])
+        return m
+
+    if later:
+        g.scalar.dma_start(T.fd[:], T.fl[:]).then_inc(S.flc, 16)
+    g.scalar.dma_start(T.fsb[:], T.fl[:]).then_inc(S.fls, 16)
+    g.sync.dma_start(T.win[:, own:own + SQ], T.st[:]).then_inc(S.stl, 16)
+    g.sync.wait_ge(S.xgo, 1)
+    g.sync.dma_start(T.win[:, 0:TC], T.x[:]).then_inc(S.xl, 16)
+
+    g.iota(T.pq[:], [[0, 8], [-1, 16]], 0, 1, allow_small_or_imprecise_dtypes=True).then_inc(S.gi, 1)
+    g.iota(T.pidx[:], [[0, 1]], 0, 1).then_inc(S.gi, 1)
+    g.iota(T.kx[:], [[16, LC]], 0, 0, allow_small_or_imprecise_dtypes=True).then_inc(S.gi, 1)
+    sent = 0
+    if later:
+        g.wait_ge(S.flc, 16)
+        m = mask(later)
+        g.remote_dma_fused([RemoteDMATransfer(
+            dst_ids=[did(r) for r in later], dma_engine_mask=m, remote_sem=S.arf, srcs=[T.fd[:]],
+            dsts=[T.flin[128 * rank:128 * rank + 128, :] for r in later])], local_sem=S.snd)
+        sent += len(engines(m))
+    g.wait_ge(S.stl, 16)
+    m = mask(near)
+    g.remote_dma_fused([RemoteDMATransfer(
+        dst_ids=[did(r) for r in near], dma_engine_mask=m, remote_sem=S.arr, srcs=[T.win[:, own:own + SQ]],
+        dsts=[T.win[:, st_place(r, rank):st_place(r, rank) + SQ] for r in near])], local_sem=S.snd)
+    sent += len(engines(m))
+    g.sem_inc(S.xgo, 1)
+
+    arr = 0
+    for r in near:
+        to = [q for q in (r + 1, r - 1) if 0 <= q < NR]
+        m = topo.mask(T.cores[r], T.cores[to[0]])
+        for q in to:
+            m &= topo.mask(T.cores[r], T.cores[q])
+        arr += len(engines(m))
+    arf = 0
+    for r in range(rank):
+        m = topo.mask(T.cores[r], T.cores[r + 1])
+        for q in range(r + 1, NR):
+            m &= topo.mask(T.cores[r], T.cores[q])
+        arf += len(engines(m))
+
+    if rank:
+        g.sync.wait_ge(S.arf, arf)
+        g.sync.dma_start(T.fe[:, 0:32 * rank], T.flin[0:128 * rank, :]).then_inc(S.fel, 16)
+
+    nv = [0]
+
+    def v(ins):
+        ins.then_inc(S.v, 1)
+        nv[0] += 1
+        g.vector.wait_ge(S.v, nv[0])
+
+    V = g.vector
+    v(V.memset(T.fb[:], 0.0))
+    v(V.memset(T.zero[:], 0.0))
+    v(V.memset(T.ones[:], 1.0))
+    V.wait_ge(S.gi, 3)
+    v(V.tensor_scalar(T.mge[:], T.pq[:], 0.0, None, AluOpType.is_ge))
+    v(V.tensor_scalar(T.mlt[:], T.pq[:], 0.0, None, AluOpType.is_lt))
+    v(V.tensor_scalar(T.meq[:], T.pq[:], 0.0, None, AluOpType.is_equal))
+    v(V.tensor_scalar(T.pmod[:], T.pidx[:], 15, None, AluOpType.bitwise_and))
+    v(V.tensor_copy(T.pmodf[:], T.pmod[:]))
+    v(V.tensor_scalar(T.kx[:], T.kx[:], T.pmodf[:], None, AluOpType.add))
+    V.wait_ge(S.fls, 16)
+    v(V.tensor_copy(T.fb[:, 1:LC + 1], T.fsb[:]))
+    g.tensor.wait_ge(S.v, nv[0])
+    g.tensor.matmul(T.pd[:, 0:LC], T.mge[:], T.fb[:, 0:LC], True, False)
+    g.tensor.matmul(T.pd[:, 0:LC], T.mlt[:], T.fb[:, 1:LC + 1], False, True).then_inc(S.t, 1)
+    g.tensor.matmul(T.pf[:, 0:LC], T.meq[:], T.fb[:, 1:LC + 1], True, True).then_inc(S.t, 1)
+    V.wait_ge(S.t, 2)
+    first = float(TC - SQ * max(rank - 1, 0))
+    v(V.tensor_tensor_scan(T.pe[:, 0:LC], T.pd[:, 0:LC], T.zero[:], first, AluOpType.add, AluOpType.add))
+    v(V.tensor_tensor(T.tb[:], T.pe[:, 0:LC], T.kx[:], AluOpType.subtract))
+    v(V.tensor_tensor(T.pe[:, 0:LC], T.tb[:], T.pf[:, 0:LC], AluOpType.mult))
+    v(V.tensor_tensor(T.hh[:], T.kx[:], T.pe[:, 0:LC], AluOpType.add))
+    if rank:
+        V.wait_ge(S.fel, 16)
+        v(V.tensor_copy(T.fef[:, 0:32 * rank], T.fe[:, 0:32 * rank]))
+        v(V.tensor_reduce(T.fes[:], T.fef[:, 0:32 * rank], AxisListType.X, AluOpType.add))
+        g.tensor.wait_ge(S.v, nv[0])
+        g.tensor.matmul(T.pc[:, 0:1], T.ones[:], T.fes[:], True, True).then_inc(S.tc, 1)
+        V.wait_ge(S.tc, 1)
+        v(V.tensor_scalar(T.pd[:, 0:LC], T.pf[:, 0:LC], T.pc[:, 0:1], None, AluOpType.mult))
+        v(V.tensor_tensor(T.hh[:], T.hh[:], T.pd[:, 0:LC], AluOpType.add))
+    v(V.tensor_copy(T.off[:], T.hh[:]))
+
+    g.scalar.wait_ge(S.v, nv[0])
+    for q in (V, g.scalar):
+        q.wait_ge(S.stl, 16)
+        q.wait_ge(S.xl, 16)
+        q.wait_ge(S.arr, arr)
+    a = 0
+    for k, n in enumerate(ROUNDS):
+        h = n // 2
+        o = S["o%d" % k]
+        V.tensor_copy(T.ot[:, a:a + h], T.win[:, 0:W].indirect(T.off[:, a // 16:(a + h) // 16])).then_inc(o, 1)
+        g.scalar.activation(T.ot[:, a + h:a + n], T.win[:, 0:W].indirect(T.off[:, (a + h) // 16:(a + n) // 16]),
+                            ActivationFunctionType.Copy).then_inc(o, 1)
+        g.sync.wait_ge(o, 2)
+        g.sync.dma_start(T.y[:, a:a + n], T.ot[:, a:a + n]).then_inc(S.ys, 16)
+        a += n
+    g.sync.wait_ge(S.ys, 16 * len(ROUNDS))
+    g.wait_ge(S.snd, sent)

@@ -4,11 +4,13 @@ from concourse.mybir import AluOpType, AxisListType, ActivationFunctionType
 NR = 6
 TC, SQ = 4096, 2048
 LC = TC // 16
+HC = 640
 ROUNDS = [1536, 1536, 1024]
 
 SCRATCH = {
     "win": ("sbuf", [128, TC + 3 * SQ], "bfloat16"),
     "ot": ("sbuf", [128, TC], "bfloat16"),
+    "hb": ("sbuf", [128, HC], "bfloat16"),
     "fsb": ("sbuf", [16, LC], "int32"),
     "fb": ("sbuf", [16, LC + 16], "bfloat16"),
     "pq": ("sbuf", [16, 128], "float32"),
@@ -34,7 +36,8 @@ SCRATCH = {
     "pe": ("psum", [128, 512], "float32"),
     "pc": ("psum", [128, 512], "float32"),
 }
-SEMAPHORES = ["flc", "fls", "stl", "xl", "xgo", "arr", "arf", "fel", "snd", "gi", "v", "t", "tc", "o0", "o1", "o2", "ys"]
+SEMAPHORES = ["flc", "fls", "sta", "stl", "har", "xl", "xgo", "arr", "arf", "fel", "snd", "gi", "v", "t", "tc",
+              "o0", "o1", "o2", "ys"]
 
 
 def engines(mask):
@@ -45,30 +48,61 @@ def st_place(rank, src):
     return TC + SQ * (src - max(rank - 1, 0))
 
 
+def near_of(rank):
+    return [r for r in (rank + 1, rank - 1) if 0 <= r < NR]
+
+
+def mask_to(topo, src, dsts):
+    m = topo.mask(src, dsts[0])
+    for d in dsts:
+        m &= topo.mask(src, d)
+    return m
+
+
+def dst_ids(topo, src, dsts):
+    return [DstId(rid=a[0], pnc=a[1]) for a in [topo.addr(d, src) for d in dsts]]
+
+
+def helper_of(topo, cores, rank):
+    me = cores[rank]
+    for c in range(me - 16, me + 16):
+        if c >= 0 and (topo.host(c), topo.chip(c)) == (topo.host(me), topo.chip(me)) and topo.die(c) != topo.die(me):
+            if all(topo.may_write(c, cores[r]) for r in range(NR) if r != rank):
+                return c
+
+
+def helper_program(g, core, T, topo, rank, n_in):
+    near = near_of(rank)
+    to = [T.cores[r] for r in near]
+    m = mask_to(topo, core, to)
+    g.wait_ge(T.sem.har, n_in)
+    g.remote_dma_fused([RemoteDMATransfer(
+        dst_ids=dst_ids(topo, core, to), dma_engine_mask=m, remote_sem=T.sem.arr, srcs=[T.hb[:]],
+        dsts=[T.win[:, st_place(r, rank):st_place(r, rank) + HC] for r in near])], local_sem=T.sem.snd)
+    g.wait_ge(T.sem.snd, len(engines(m)))
+
+
 def rank_program(g, core, T, topo):
+    helpers = [helper_of(topo, T.cores, r) for r in range(NR)]
+    hmask = [topo.mask(T.cores[r], helpers[r]) & ~mask_to(topo, T.cores[r], [T.cores[q] for q in near_of(r)])
+             for r in range(NR)]
     rank = T.rank_of(core)
     if rank is None:
+        if core in helpers:
+            r = helpers.index(core)
+            helper_program(g, core, T, topo, r, len(engines(hmask[r])))
         return
     S = T.sem
     W = TC + SQ * (3 - (rank == 0) - (rank == NR - 1))
     own = st_place(rank, rank)
-    near = [r for r in (rank + 1, rank - 1) if 0 <= r < NR]
+    near = near_of(rank)
     later = list(range(rank + 1, NR))
-
-    def did(r):
-        rid, pid = topo.addr(T.cores[r], core)
-        return DstId(rid=rid, pnc=pid)
-
-    def mask(rs):
-        m = topo.mask(core, T.cores[rs[0]])
-        for r in rs:
-            m &= topo.mask(core, T.cores[r])
-        return m
 
     if later:
         g.scalar.dma_start(T.fd[:], T.fl[:]).then_inc(S.flc, 16)
     g.scalar.dma_start(T.fsb[:], T.fl[:]).then_inc(S.fls, 16)
-    g.sync.dma_start(T.win[:, own:own + SQ], T.st[:]).then_inc(S.stl, 16)
+    g.sync.dma_start(T.win[:, own:own + HC], T.st[:, 0:HC]).then_inc(S.sta, 16)
+    g.sync.dma_start(T.win[:, own + HC:own + SQ], T.st[:, HC:SQ]).then_inc(S.stl, 16)
     g.sync.wait_ge(S.xgo, 1)
     g.sync.dma_start(T.win[:, 0:TC], T.x[:]).then_inc(S.xl, 16)
 
@@ -77,33 +111,31 @@ def rank_program(g, core, T, topo):
     g.iota(T.kx[:], [[16, LC]], 0, 0, allow_small_or_imprecise_dtypes=True).then_inc(S.gi, 1)
     sent = 0
     if later:
+        to = [T.cores[r] for r in later]
+        m = mask_to(topo, core, to)
         g.wait_ge(S.flc, 16)
-        m = mask(later)
         g.remote_dma_fused([RemoteDMATransfer(
-            dst_ids=[did(r) for r in later], dma_engine_mask=m, remote_sem=S.arf, srcs=[T.fd[:]],
+            dst_ids=dst_ids(topo, core, to), dma_engine_mask=m, remote_sem=S.arf, srcs=[T.fd[:]],
             dsts=[T.flin[128 * rank:128 * rank + 128, :] for r in later])], local_sem=S.snd)
         sent += len(engines(m))
+    g.wait_ge(S.sta, 16)
+    rid, pid = topo.addr(helpers[rank], core)
+    g.remote_dma(T.hb[:], T.win[:, own:own + HC], S.har, S.snd, pid, rid, hmask[rank])
+    sent += len(engines(hmask[rank]))
+    to = [T.cores[r] for r in near]
+    m = mask_to(topo, core, to)
     g.wait_ge(S.stl, 16)
-    m = mask(near)
     g.remote_dma_fused([RemoteDMATransfer(
-        dst_ids=[did(r) for r in near], dma_engine_mask=m, remote_sem=S.arr, srcs=[T.win[:, own:own + SQ]],
-        dsts=[T.win[:, st_place(r, rank):st_place(r, rank) + SQ] for r in near])], local_sem=S.snd)
+        dst_ids=dst_ids(topo, core, to), dma_engine_mask=m, remote_sem=S.arr, srcs=[T.win[:, own + HC:own + SQ]],
+        dsts=[T.win[:, st_place(r, rank) + HC:st_place(r, rank) + SQ] for r in near])], local_sem=S.snd)
     sent += len(engines(m))
     g.sem_inc(S.xgo, 1)
 
     arr = 0
     for r in near:
-        to = [q for q in (r + 1, r - 1) if 0 <= q < NR]
-        m = topo.mask(T.cores[r], T.cores[to[0]])
-        for q in to:
-            m &= topo.mask(T.cores[r], T.cores[q])
-        arr += len(engines(m))
-    arf = 0
-    for r in range(rank):
-        m = topo.mask(T.cores[r], T.cores[r + 1])
-        for q in range(r + 1, NR):
-            m &= topo.mask(T.cores[r], T.cores[q])
-        arf += len(engines(m))
+        to = [T.cores[q] for q in near_of(r)]
+        arr += len(engines(mask_to(topo, T.cores[r], to))) + len(engines(mask_to(topo, helpers[r], to)))
+    arf = sum(len(engines(mask_to(topo, T.cores[r], T.cores[r + 1:]))) for r in range(rank))
 
     if rank:
         g.sync.wait_ge(S.arf, arf)
@@ -152,6 +184,7 @@ def rank_program(g, core, T, topo):
 
     g.scalar.wait_ge(S.v, nv[0])
     for q in (V, g.scalar):
+        q.wait_ge(S.sta, 16)
         q.wait_ge(S.stl, 16)
         q.wait_ge(S.xl, 16)
         q.wait_ge(S.arr, arr)

@@ -4,13 +4,17 @@ from concourse.mybir import AluOpType, AxisListType, ActivationFunctionType
 NR = 6
 TC, SQ = 4096, 2048
 LC = TC // 16
-HC = 640
+HS = [480, 368]
+HC = sum(HS)
+HO = [0, HS[0]]
+XE = 1792
+KH = LC // len(HS)
 ROUNDS = [1536, 1536, 1024]
 
 SCRATCH = {
     "win": ("sbuf", [128, TC + 3 * SQ], "bfloat16"),
     "ot": ("sbuf", [128, TC], "bfloat16"),
-    "hb": ("sbuf", [128, HC], "bfloat16"),
+    "hb": ("sbuf", [128, max(HS)], "bfloat16"),
     "fsb": ("sbuf", [16, LC], "int32"),
     "fb": ("sbuf", [16, LC + 16], "bfloat16"),
     "pq": ("sbuf", [16, 128], "float32"),
@@ -36,8 +40,8 @@ SCRATCH = {
     "pe": ("psum", [128, 512], "float32"),
     "pc": ("psum", [128, 512], "float32"),
 }
-SEMAPHORES = ["flc", "fls", "sta", "stl", "har", "xl", "xgo", "arr", "arf", "fel", "snd", "gi", "v", "t", "tc",
-              "o0", "o1", "o2", "ys"]
+SEMAPHORES = ["flc", "fls", "st0", "st1", "stl", "har", "tab", "xe", "xl", "xgo", "arr", "arf", "fel", "snd", "gi", "v", "t",
+              "tc", "o0", "o1", "o2", "ys"]
 
 
 def engines(mask):
@@ -63,34 +67,49 @@ def dst_ids(topo, src, dsts):
     return [DstId(rid=a[0], pnc=a[1]) for a in [topo.addr(d, src) for d in dsts]]
 
 
-def helper_of(topo, cores, rank):
-    me = cores[rank]
+def helpers_of(topo, cores, rank):
+    me, out = cores[rank], []
     for c in range(me - 16, me + 16):
         if c >= 0 and (topo.host(c), topo.chip(c)) == (topo.host(me), topo.chip(me)) and topo.die(c) != topo.die(me):
             if all(topo.may_write(c, cores[r]) for r in range(NR) if r != rank):
-                return c
+                out.append(c)
+    return out[:len(HS)]
 
 
-def helper_program(g, core, T, topo, rank, n_in):
+def helper_program(g, core, T, topo, rank, k, n_in):
     near = near_of(rank)
     to = [T.cores[r] for r in near]
     m = mask_to(topo, core, to)
-    g.wait_ge(T.sem.har, n_in)
+    V, S = g.vector, T.sem
+    c = KH * k
+    g.iota(T.pidx[:], [[0, 1]], 0, 1).then_inc(S.gi, 1)
+    g.iota(T.kx[:, c:c + KH], [[16, KH]], 16 * c, 0, allow_small_or_imprecise_dtypes=True).then_inc(S.gi, 1)
+    V.wait_ge(S.gi, 2)
+    V.tensor_scalar(T.pmod[:], T.pidx[:], 15, None, AluOpType.bitwise_and).then_inc(S.v, 1)
+    V.wait_ge(S.v, 1)
+    V.tensor_copy(T.pmodf[:], T.pmod[:]).then_inc(S.v, 1)
+    V.wait_ge(S.v, 2)
+    V.tensor_scalar(T.kx[:, c:c + KH], T.kx[:, c:c + KH], T.pmodf[:], None, AluOpType.add).then_inc(S.v, 1)
+    g.wait_ge(S.v, 3)
+    rid, pid = topo.addr(T.cores[rank], core)
+    g.remote_dma(T.kx[:, c:c + KH], T.kx[:, c:c + KH], S.tab, S.snd, pid, rid, m)
+    g.wait_ge(S.har, n_in)
+    h, o = HS[k], HO[k]
     g.remote_dma_fused([RemoteDMATransfer(
-        dst_ids=dst_ids(topo, core, to), dma_engine_mask=m, remote_sem=T.sem.arr, srcs=[T.hb[:]],
-        dsts=[T.win[:, st_place(r, rank):st_place(r, rank) + HC] for r in near])], local_sem=T.sem.snd)
-    g.wait_ge(T.sem.snd, len(engines(m)))
+        dst_ids=dst_ids(topo, core, to), dma_engine_mask=m, remote_sem=S.arr, srcs=[T.hb[:, 0:h]],
+        dsts=[T.win[:, st_place(r, rank) + o:st_place(r, rank) + o + h] for r in near])], local_sem=S.snd)
+    g.wait_ge(S.snd, 2 * len(engines(m)))
 
 
 def rank_program(g, core, T, topo):
-    helpers = [helper_of(topo, T.cores, r) for r in range(NR)]
-    hmask = [topo.mask(T.cores[r], helpers[r]) & ~mask_to(topo, T.cores[r], [T.cores[q] for q in near_of(r)])
+    helpers = [helpers_of(topo, T.cores, r) for r in range(NR)]
+    hmask = [topo.mask(T.cores[r], helpers[r][0]) & ~mask_to(topo, T.cores[r], [T.cores[q] for q in near_of(r)])
              for r in range(NR)]
     rank = T.rank_of(core)
     if rank is None:
-        if core in helpers:
-            r = helpers.index(core)
-            helper_program(g, core, T, topo, r, len(engines(hmask[r])))
+        for r in range(NR):
+            if core in helpers[r]:
+                helper_program(g, core, T, topo, r, helpers[r].index(core), len(engines(hmask[r])))
         return
     S = T.sem
     W = TC + SQ * (3 - (rank == 0) - (rank == NR - 1))
@@ -101,14 +120,14 @@ def rank_program(g, core, T, topo):
     if later:
         g.scalar.dma_start(T.fd[:], T.fl[:]).then_inc(S.flc, 16)
     g.scalar.dma_start(T.fsb[:], T.fl[:]).then_inc(S.fls, 16)
-    g.sync.dma_start(T.win[:, own:own + HC], T.st[:, 0:HC]).then_inc(S.sta, 16)
+    for k, (o, h) in enumerate(zip(HO, HS)):
+        g.sync.dma_start(T.win[:, own + o:own + o + h], T.st[:, o:o + h]).then_inc(S["st%d" % k], 16)
     g.sync.dma_start(T.win[:, own + HC:own + SQ], T.st[:, HC:SQ]).then_inc(S.stl, 16)
+    g.sync.dma_start(T.win[:, 0:XE], T.x[:, 0:XE]).then_inc(S.xe, 16)
     g.sync.wait_ge(S.xgo, 1)
-    g.sync.dma_start(T.win[:, 0:TC], T.x[:]).then_inc(S.xl, 16)
+    g.sync.dma_start(T.win[:, XE:TC], T.x[:, XE:TC]).then_inc(S.xl, 16)
 
     g.iota(T.pq[:], [[0, 8], [-1, 16]], 0, 1, allow_small_or_imprecise_dtypes=True).then_inc(S.gi, 1)
-    g.iota(T.pidx[:], [[0, 1]], 0, 1).then_inc(S.gi, 1)
-    g.iota(T.kx[:], [[16, LC]], 0, 0, allow_small_or_imprecise_dtypes=True).then_inc(S.gi, 1)
     sent = 0
     if later:
         to = [T.cores[r] for r in later]
@@ -118,10 +137,11 @@ def rank_program(g, core, T, topo):
             dst_ids=dst_ids(topo, core, to), dma_engine_mask=m, remote_sem=S.arf, srcs=[T.fd[:]],
             dsts=[T.flin[128 * rank:128 * rank + 128, :] for r in later])], local_sem=S.snd)
         sent += len(engines(m))
-    g.wait_ge(S.sta, 16)
-    rid, pid = topo.addr(helpers[rank], core)
-    g.remote_dma(T.hb[:], T.win[:, own:own + HC], S.har, S.snd, pid, rid, hmask[rank])
-    sent += len(engines(hmask[rank]))
+    for k, (o, h) in enumerate(zip(HO, HS)):
+        g.wait_ge(S["st%d" % k], 16)
+        rid, pid = topo.addr(helpers[rank][k], core)
+        g.remote_dma(T.hb[:, 0:h], T.win[:, own + o:own + o + h], S.har, S.snd, pid, rid, hmask[rank])
+        sent += len(engines(hmask[rank]))
     to = [T.cores[r] for r in near]
     m = mask_to(topo, core, to)
     g.wait_ge(S.stl, 16)
@@ -134,7 +154,8 @@ def rank_program(g, core, T, topo):
     arr = 0
     for r in near:
         to = [T.cores[q] for q in near_of(r)]
-        arr += len(engines(mask_to(topo, T.cores[r], to))) + len(engines(mask_to(topo, helpers[r], to)))
+        arr += sum(len(engines(mask_to(topo, c, to))) for c in [T.cores[r]] + helpers[r])
+    tab = sum(len(engines(mask_to(topo, c, [T.cores[r] for r in near]))) for c in helpers[rank])
     arf = sum(len(engines(mask_to(topo, T.cores[r], T.cores[r + 1:]))) for r in range(rank))
 
     if rank:
@@ -152,13 +173,10 @@ def rank_program(g, core, T, topo):
     v(V.memset(T.fb[:], 0.0))
     v(V.memset(T.zero[:], 0.0))
     v(V.memset(T.ones[:], 1.0))
-    V.wait_ge(S.gi, 3)
+    V.wait_ge(S.gi, 1)
     v(V.tensor_scalar(T.mge[:], T.pq[:], 0.0, None, AluOpType.is_ge))
     v(V.tensor_scalar(T.mlt[:], T.pq[:], 0.0, None, AluOpType.is_lt))
     v(V.tensor_scalar(T.meq[:], T.pq[:], 0.0, None, AluOpType.is_equal))
-    v(V.tensor_scalar(T.pmod[:], T.pidx[:], 15, None, AluOpType.bitwise_and))
-    v(V.tensor_copy(T.pmodf[:], T.pmod[:]))
-    v(V.tensor_scalar(T.kx[:], T.kx[:], T.pmodf[:], None, AluOpType.add))
     V.wait_ge(S.fls, 16)
     v(V.tensor_copy(T.fb[:, 1:LC + 1], T.fsb[:]))
     g.tensor.wait_ge(S.v, nv[0])
@@ -168,6 +186,7 @@ def rank_program(g, core, T, topo):
     V.wait_ge(S.t, 2)
     first = float(TC - SQ * max(rank - 1, 0))
     v(V.tensor_tensor_scan(T.pe[:, 0:LC], T.pd[:, 0:LC], T.zero[:], first, AluOpType.add, AluOpType.add))
+    V.wait_ge(S.tab, tab)
     v(V.tensor_tensor(T.tb[:], T.pe[:, 0:LC], T.kx[:], AluOpType.subtract))
     v(V.tensor_tensor(T.pe[:, 0:LC], T.tb[:], T.pf[:, 0:LC], AluOpType.mult))
     v(V.tensor_tensor(T.hh[:], T.kx[:], T.pe[:, 0:LC], AluOpType.add))
@@ -184,9 +203,8 @@ def rank_program(g, core, T, topo):
 
     g.scalar.wait_ge(S.v, nv[0])
     for q in (V, g.scalar):
-        q.wait_ge(S.sta, 16)
-        q.wait_ge(S.stl, 16)
-        q.wait_ge(S.xl, 16)
+        for w in (S.st0, S.st1, S.stl, S.xe, S.xl):
+            q.wait_ge(w, 16)
         q.wait_ge(S.arr, arr)
     a = 0
     for k, n in enumerate(ROUNDS):

from concourse.bass import DstId, RemoteDMATransfer
from concourse.mybir import AluOpType, AxisListType, ActivationFunctionType

NR = 6
TC, SQ = 4096, 2048
LC = TC // 16
HS = [480, 368]
HC = sum(HS)
HO = [0, HS[0]]
XE = 1792
KH = LC // len(HS)
ROUNDS = [1536, 1536, 1024]

SCRATCH = {
    "win": ("sbuf", [128, TC + 3 * SQ], "bfloat16"),
    "ot": ("sbuf", [128, TC], "bfloat16"),
    "hb": ("sbuf", [128, max(HS)], "bfloat16"),
    "fsb": ("sbuf", [16, LC], "int32"),
    "fb": ("sbuf", [16, LC + 16], "bfloat16"),
    "pq": ("sbuf", [16, 128], "float32"),
    "mge": ("sbuf", [16, 128], "bfloat16"),
    "mlt": ("sbuf", [16, 128], "bfloat16"),
    "meq": ("sbuf", [16, 128], "bfloat16"),
    "pidx": ("sbuf", [128, 1], "int32"),
    "pmod": ("sbuf", [128, 1], "int32"),
    "pmodf": ("sbuf", [128, 1], "float32"),
    "kx": ("sbuf", [128, LC], "float32"),
    "zero": ("sbuf", [128, LC], "float32"),
    "ones": ("sbuf", [128, 128], "float32"),
    "tb": ("sbuf", [128, LC], "float32"),
    "hh": ("sbuf", [128, LC], "float32"),
    "off": ("sbuf", [128, LC], "uint16"),
    "fe": ("sbuf", [128, 32 * (NR - 1)], "int32"),
    "fef": ("sbuf", [128, 32 * (NR - 1)], "bfloat16"),
    "fes": ("sbuf", [128, 1], "float32"),
    "fd": ("dram", [128, 32], "int32"),
    "flin": ("dram", [128 * (NR - 1), 32], "int32"),
    "pd": ("psum", [128, 512], "float32"),
    "pf": ("psum", [128, 512], "float32"),
    "pe": ("psum", [128, 512], "float32"),
    "pc": ("psum", [128, 512], "float32"),
}
SEMAPHORES = ["flc", "fls", "st0", "st1", "stl", "har", "tab", "xe", "xl", "xgo", "arr", "arf", "fel", "snd", "gi", "v", "t",
              "tc", "o0", "o1", "o2", "ys"]


def engines(mask):
    return [i for i in range(16) if (mask >> i) & 1]


def st_place(rank, src):
    return TC + SQ * (src - max(rank - 1, 0))


def near_of(rank):
    return [r for r in (rank + 1, rank - 1) if 0 <= r < NR]


def mask_to(topo, src, dsts):
    m = topo.mask(src, dsts[0])
    for d in dsts:
        m &= topo.mask(src, d)
    return m


def dst_ids(topo, src, dsts):
    return [DstId(rid=a[0], pnc=a[1]) for a in [topo.addr(d, src) for d in dsts]]


def helpers_of(topo, cores, rank):
    me, out = cores[rank], []
    for c in range(me - 16, me + 16):
        if c >= 0 and (topo.host(c), topo.chip(c)) == (topo.host(me), topo.chip(me)) and topo.die(c) != topo.die(me):
            if all(topo.may_write(c, cores[r]) for r in range(NR) if r != rank):
                out.append(c)
    return out[:len(HS)]


def helper_program(g, core, T, topo, rank, k, n_in):
    near = near_of(rank)
    to = [T.cores[r] for r in near]
    m = mask_to(topo, core, to)
    V, S = g.vector, T.sem
    c = KH * k
    g.iota(T.pidx[:], [[0, 1]], 0, 1).then_inc(S.gi, 1)
    g.iota(T.kx[:, c:c + KH], [[16, KH]], 16 * c, 0, allow_small_or_imprecise_dtypes=True).then_inc(S.gi, 1)
    V.wait_ge(S.gi, 2)
    V.tensor_scalar(T.pmod[:], T.pidx[:], 15, None, AluOpType.bitwise_and).then_inc(S.v, 1)
    V.wait_ge(S.v, 1)
    V.tensor_copy(T.pmodf[:], T.pmod[:]).then_inc(S.v, 1)
    V.wait_ge(S.v, 2)
    V.tensor_scalar(T.kx[:, c:c + KH], T.kx[:, c:c + KH], T.pmodf[:], None, AluOpType.add).then_inc(S.v, 1)
    g.wait_ge(S.v, 3)
    rid, pid = topo.addr(T.cores[rank], core)
    g.remote_dma(T.kx[:, c:c + KH], T.kx[:, c:c + KH], S.tab, S.snd, pid, rid, m)
    g.wait_ge(S.har, n_in)
    h, o = HS[k], HO[k]
    g.remote_dma_fused([RemoteDMATransfer(
        dst_ids=dst_ids(topo, core, to), dma_engine_mask=m, remote_sem=S.arr, srcs=[T.hb[:, 0:h]],
        dsts=[T.win[:, st_place(r, rank) + o:st_place(r, rank) + o + h] for r in near])], local_sem=S.snd)
    g.wait_ge(S.snd, 2 * len(engines(m)))


def rank_program(g, core, T, topo):
    helpers = [helpers_of(topo, T.cores, r) for r in range(NR)]
    hmask = [topo.mask(T.cores[r], helpers[r][0]) & ~mask_to(topo, T.cores[r], [T.cores[q] for q in near_of(r)])
             for r in range(NR)]
    rank = T.rank_of(core)
    if rank is None:
        for r in range(NR):
            if core in helpers[r]:
                helper_program(g, core, T, topo, r, helpers[r].index(core), len(engines(hmask[r])))
        return
    S = T.sem
    W = TC + SQ * (3 - (rank == 0) - (rank == NR - 1))
    own = st_place(rank, rank)
    near = near_of(rank)
    later = list(range(rank + 1, NR))

    if later:
        g.scalar.dma_start(T.fd[:], T.fl[:]).then_inc(S.flc, 16)
    g.scalar.dma_start(T.fsb[:], T.fl[:]).then_inc(S.fls, 16)
    for k, (o, h) in enumerate(zip(HO, HS)):
        g.sync.dma_start(T.win[:, own + o:own + o + h], T.st[:, o:o + h]).then_inc(S["st%d" % k], 16)
    g.sync.dma_start(T.win[:, own + HC:own + SQ], T.st[:, HC:SQ]).then_inc(S.stl, 16)
    g.sync.dma_start(T.win[:, 0:XE], T.x[:, 0:XE]).then_inc(S.xe, 16)
    g.sync.wait_ge(S.xgo, 1)
    g.sync.dma_start(T.win[:, XE:TC], T.x[:, XE:TC]).then_inc(S.xl, 16)

    g.iota(T.pq[:], [[0, 8], [-1, 16]], 0, 1, allow_small_or_imprecise_dtypes=True).then_inc(S.gi, 1)
    sent = 0
    if later:
        to = [T.cores[r] for r in later]
        m = mask_to(topo, core, to)
        g.wait_ge(S.flc, 16)
        g.remote_dma_fused([RemoteDMATransfer(
            dst_ids=dst_ids(topo, core, to), dma_engine_mask=m, remote_sem=S.arf, srcs=[T.fd[:]],
            dsts=[T.flin[128 * rank:128 * rank + 128, :] for r in later])], local_sem=S.snd)
        sent += len(engines(m))
    for k, (o, h) in enumerate(zip(HO, HS)):
        g.wait_ge(S["st%d" % k], 16)
        rid, pid = topo.addr(helpers[rank][k], core)
        g.remote_dma(T.hb[:, 0:h], T.win[:, own + o:own + o + h], S.har, S.snd, pid, rid, hmask[rank])
        sent += len(engines(hmask[rank]))
    to = [T.cores[r] for r in near]
    m = mask_to(topo, core, to)
    g.wait_ge(S.stl, 16)
    g.remote_dma_fused([RemoteDMATransfer(
        dst_ids=dst_ids(topo, core, to), dma_engine_mask=m, remote_sem=S.arr, srcs=[T.win[:, own + HC:own + SQ]],
        dsts=[T.win[:, st_place(r, rank) + HC:st_place(r, rank) + SQ] for r in near])], local_sem=S.snd)
    sent += len(engines(m))
    g.sem_inc(S.xgo, 1)

    arr = 0
    for r in near:
        to = [T.cores[q] for q in near_of(r)]
        arr += sum(len(engines(mask_to(topo, c, to))) for c in [T.cores[r]] + helpers[r])
    tab = sum(len(engines(mask_to(topo, c, [T.cores[r] for r in near]))) for c in helpers[rank])
    arf = sum(len(engines(mask_to(topo, T.cores[r], T.cores[r + 1:]))) for r in range(rank))

    if rank:
        g.sync.wait_ge(S.arf, arf)
        g.sync.dma_start(T.fe[:, 0:32 * rank], T.flin[0:128 * rank, :]).then_inc(S.fel, 16)

    nv = [0]

    def v(ins):
        ins.then_inc(S.v, 1)
        nv[0] += 1
        g.vector.wait_ge(S.v, nv[0])

    V = g.vector
    v(V.memset(T.fb[:], 0.0))
    v(V.memset(T.zero[:], 0.0))
    v(V.memset(T.ones[:], 1.0))
    V.wait_ge(S.gi, 1)
    v(V.tensor_scalar(T.mge[:], T.pq[:], 0.0, None, AluOpType.is_ge))
    v(V.tensor_scalar(T.mlt[:], T.pq[:], 0.0, None, AluOpType.is_lt))
    v(V.tensor_scalar(T.meq[:], T.pq[:], 0.0, None, AluOpType.is_equal))
    V.wait_ge(S.fls, 16)
    v(V.tensor_copy(T.fb[:, 1:LC + 1], T.fsb[:]))
    g.tensor.wait_ge(S.v, nv[0])
    g.tensor.matmul(T.pd[:, 0:LC], T.mge[:], T.fb[:, 0:LC], True, False)
    g.tensor.matmul(T.pd[:, 0:LC], T.mlt[:], T.fb[:, 1:LC + 1], False, True).then_inc(S.t, 1)
    g.tensor.matmul(T.pf[:, 0:LC], T.meq[:], T.fb[:, 1:LC + 1], True, True).then_inc(S.t, 1)
    V.wait_ge(S.t, 2)
    first = float(TC - SQ * max(rank - 1, 0))
    v(V.tensor_tensor_scan(T.pe[:, 0:LC], T.pd[:, 0:LC], T.zero[:], first, AluOpType.add, AluOpType.add))
    V.wait_ge(S.tab, tab)
    v(V.tensor_tensor(T.tb[:], T.pe[:, 0:LC], T.kx[:], AluOpType.subtract))
    v(V.tensor_tensor(T.pe[:, 0:LC], T.tb[:], T.pf[:, 0:LC], AluOpType.mult))
    v(V.tensor_tensor(T.hh[:], T.kx[:], T.pe[:, 0:LC], AluOpType.add))
    if rank:
        V.wait_ge(S.fel, 16)
        v(V.tensor_copy(T.fef[:, 0:32 * rank], T.fe[:, 0:32 * rank]))
        v(V.tensor_reduce(T.fes[:], T.fef[:, 0:32 * rank], AxisListType.X, AluOpType.add))
        g.tensor.wait_ge(S.v, nv[0])
        g.tensor.matmul(T.pc[:, 0:1], T.ones[:], T.fes[:], True, True).then_inc(S.tc, 1)
        V.wait_ge(S.tc, 1)
        v(V.tensor_scalar(T.pd[:, 0:LC], T.pf[:, 0:LC], T.pc[:, 0:1], None, AluOpType.mult))
        v(V.tensor_tensor(T.hh[:], T.hh[:], T.pd[:, 0:LC], AluOpType.add))
    v(V.tensor_copy(T.off[:], T.hh[:]))

    g.scalar.wait_ge(S.v, nv[0])
    for q in (V, g.scalar):
        for w in (S.st0, S.st1, S.stl, S.xe, S.xl):
            q.wait_ge(w, 16)
        q.wait_ge(S.arr, arr)
    a = 0
    for k, n in enumerate(ROUNDS):
        h = n // 2
        o = S["o%d" % k]
        V.tensor_copy(T.ot[:, a:a + h], T.win[:, 0:W].indirect(T.off[:, a // 16:(a + h) // 16])).then_inc(o, 1)
        g.scalar.activation(T.ot[:, a + h:a + n], T.win[:, 0:W].indirect(T.off[:, (a + h) // 16:(a + n) // 16]),
                            ActivationFunctionType.Copy).then_inc(o, 1)
        g.sync.wait_ge(o, 2)
        g.sync.dma_start(T.y[:, a:a + n], T.ot[:, a:a + n]).then_inc(S.ys, 16)
        a += n
    g.sync.wait_ge(S.ys, 16 * len(ROUNDS))
    g.wait_ge(S.snd, sent)
